import numpy as np, ml_dtypes
CORES = [7,391,135,263,15,399,143,271]
N = 8
KT, C = 4, 128
def setup_inputs(rng):
    return {"x": rng.standard_normal((N, 128, KT * C), dtype=np.float32).astype(ml_dtypes.bfloat16)}
def setup_inputs_big(rng):
    d = setup_inputs(rng)
    for k in ("x",): d[k] = (d[k].astype(np.float32) * 1024.0).astype(d[k].dtype)
    return d
def setup_inputs_small(rng):
    d = setup_inputs(rng)
    for k in ("x",): d[k] = (d[k].astype(np.float32) * (1 / 1024.0)).astype(d[k].dtype)
    return d
def setup_inputs_apart(rng):
    d = setup_inputs(rng)
    f = (10.0 ** rng.permutation(np.linspace(-1.5, 1.5, N))).astype(np.float32).reshape(N, 1, 1)
    for k in ("x",): d[k] = (d[k].astype(np.float32) * f).astype(d[k].dtype)
    return d
def reference(x):
    X = x.astype(np.float64)
    y = np.full((N, C, N * C), np.nan)
    for r in range(N):
        for i in range(N):
            s = i
            if s != r: y[r][:, C * i:C * i + C] = sum(X[r][:, C * t:C * t + C].T @ X[s][:, C * t:C * t + C] for t in range(KT))
    return {"y": y.astype(ml_dtypes.bfloat16 if x.dtype != np.float64 else np.float64)}

@@ -1,0 +1,136 @@
+from concourse.bass import DstId, RemoteDMATransfer
+
+KT, C = 4, 128
+W = KT * C
+
+SCRATCH = {
+    "xs": ("sbuf", [128, W], "bfloat16"),
+    "xp": ("sbuf", [128, W], "bfloat16"),
+    "xn0": ("sbuf", [128, W], "bfloat16"),
+    "xn1": ("sbuf", [128, W], "bfloat16"),
+    "sam": ("sbuf", [128, 2 * C], "bfloat16"),
+    "sd": ("sbuf", [128, 2 * C], "bfloat16"),
+    "lam": ("sbuf", [128, 2 * C], "bfloat16"),
+    "ldd": ("sbuf", [128, 2 * C], "bfloat16"),
+    "yb": ("sbuf", [128, 8 * C], "bfloat16"),
+    "pam": ("psum", [128, 512], "float32"),
+    "pd0": ("psum", [128, 512], "float32"),
+    "pd1": ("psum", [128, 512], "float32"),
+    "po0": ("psum", [128, 512], "float32"),
+    "po1": ("psum", [128, 512], "float32"),
+    "po2": ("psum", [128, 512], "float32"),
+}
+SEMAPHORES = ["ld", "sb", "sa", "snt", "mam", "md0", "md1", "mo0", "mo1", "mo2", "cam", "cd", "sg1", "sg2", "ybs", "st"]
+
+
+def _plan(core, cores, topo):
+    hosts = sorted({topo.host(c) for c in cores})
+    chips = sorted({topo.chip(c) for c in cores})
+    at = {(topo.host(c), topo.chip(c)): c for c in cores}
+
+    def linked(a, b):
+        return a != b and all(topo.may_write(at[(a, k)], at[(b, k)]) for k in chips)
+
+    ring = [hosts[0]]
+    ring.append([h for h in hosts if linked(ring[0], h) and topo.rack(h) == topo.rack(ring[0])][0])
+    while len(ring) < len(hosts):
+        ring.append([h for h in hosts if linked(ring[-1], h) and h not in ring][0])
+    i = ring.index(topo.host(core))
+    nxt, prv, far = ring[(i + 1) % len(ring)], ring[i - 1], ring[(i + 2) % len(ring)]
+    me_h, c = topo.host(core), topo.chip(core)
+    oc = [k for k in chips if k != c][0]
+    return {
+        "slot": chips.index(c),
+        "prev_same": at[(prv, c)], "prev_other": at[(prv, oc)],
+        "next_same": at[(nxt, c)], "next_other": at[(nxt, oc)],
+        "next_lo": at[(nxt, chips[0])], "next_hi": at[(nxt, chips[1])],
+        "far_lo": at[(far, chips[0])], "far_hi": at[(far, chips[1])],
+        "mate": at[(me_h, oc)],
+    }
+
+
+def rank_program(g, core, T, topo):
+    rank = T.rank_of(core)
+    if rank is None:
+        return
+    p = _plan(core, list(T.cores), topo)
+    S = T.sem
+
+    def tile(buf, t):
+        return buf[:, C * t:C * t + C]
+
+    def yblk(c):
+        r = T.rank_of(c)
+        return T.yb[:, C * r:C * r + C]
+
+    def gram(out, a, b, sem):
+        for t in range(KT):
+            m = g.tensor.matmul(out, tile(a, t), tile(b, t), t == 0, t == KT - 1)
+        m.then_inc(sem, 1)
+
+    def send(dst, out_ap, in_ap, sem):
+        rid, pid = topo.addr(dst, core)
+        g.remote_dma(out_ap, in_ap, sem, S.snt, pid, rid, topo.mask(core, dst))
+        return bin(topo.mask(core, dst)).count("1")
+
+    g.sync.dma_start(T.xs[:], T.x[:]).then_inc(S.ld, 16)
+
+    g.wait_ge(S.ld, 16)
+    mine = T.xn0 if p["slot"] == 0 else T.xn1
+    back = [p["prev_same"], p["prev_other"]]
+    m_back = topo.mask(core, back[0]) & topo.mask(core, back[1])
+    ids = []
+    for d in back:
+        rid, pid = topo.addr(d, core)
+        ids.append(DstId(rid=rid, pnc=pid))
+    g.remote_dma_fused([RemoteDMATransfer(dst_ids=ids, dma_engine_mask=m_back, remote_sem=S.sb,
+                                          srcs=[T.xs[:]], dsts=[mine[:], mine[:]], alu_op=0)], local_sem=S.snt)
+    left = bin(m_back).count("1")
+    left += send(p["next_same"], T.xp[:], T.xs[:], S.sa)
+    g.wait_ge(S.cam, 1)
+    left += send(p["next_other"], T.lam[:], T.sam[:], S.sg1)
+    g.wait_ge(S.cd, 2)
+    left += send(p["prev_same"], T.ldd[:], T.sd[:], S.sg2)
+    g.wait_ge(S.snt, left)
+
+    def n_in(src):
+        return bin(topo.mask(src, core)).count("1")
+    in_b = 2 * bin(topo.mask(p["next_lo"], core) & topo.mask(p["next_hi"], core)).count("1")
+
+    x_no = T.xn0 if p["next_other"] == p["next_lo"] else T.xn1
+    x_ns = T.xn0 if p["next_same"] == p["next_lo"] else T.xn1
+    g.tensor.wait_ge(S.ld, 16)
+    g.tensor.wait_ge(S.sb, in_b)
+    gram(T.pam[:, 0:C], x_no, T.xs, S.mam)
+    gram(T.pam[:, C:2 * C], x_no, x_ns, S.mam)
+    g.tensor.wait_ge(S.sa, n_in(p["prev_same"]))
+    gram(T.pd0[:, 0:C], T.xp, T.xn0, S.md0)
+    gram(T.pd1[:, 0:C], T.xp, T.xn1, S.md1)
+    gram(T.po0[:, 0:C], T.xs, T.xn0, S.mo0)
+    gram(T.po1[:, 0:C], T.xs, T.xn1, S.mo1)
+    gram(T.po2[:, 0:C], T.xs, T.xp, S.mo2)
+
+    v = g.vector
+    v.memset(yblk(core), 0.0).then_inc(S.ybs, 1)
+    v.wait_ge(S.mam, 2)
+    v.tensor_copy(T.sam[:], T.pam[:, 0:2 * C]).then_inc(S.cam, 1)
+    v.wait_ge(S.md0, 1)
+    v.tensor_copy(T.sd[:, 0:C], T.pd0[:, 0:C]).then_inc(S.cd, 1)
+    v.wait_ge(S.md1, 1)
+    v.tensor_copy(T.sd[:, C:2 * C], T.pd1[:, 0:C]).then_inc(S.cd, 1)
+    v.wait_ge(S.mo0, 1)
+    v.tensor_copy(yblk(p["next_lo"]), T.po0[:, 0:C]).then_inc(S.ybs, 1)
+    v.wait_ge(S.mo1, 1)
+    v.tensor_copy(yblk(p["next_hi"]), T.po1[:, 0:C]).then_inc(S.ybs, 1)
+    v.wait_ge(S.mo2, 1)
+    v.tensor_copy(yblk(p["prev_same"]), T.po2[:, 0:C]).then_inc(S.ybs, 1)
+    v.wait_ge(S.sg1, n_in(p["prev_other"]))
+    v.tensor_copy(yblk(p["prev_other"]), T.lam[:, 0:C]).then_inc(S.ybs, 1)
+    v.tensor_copy(yblk(p["mate"]), T.lam[:, C:2 * C]).then_inc(S.ybs, 1)
+    v.wait_ge(S.sg2, n_in(p["next_same"]))
+    v.tensor_copy(yblk(p["far_lo"]), T.ldd[:, 0:C]).then_inc(S.ybs, 1)
+    v.tensor_copy(yblk(p["far_hi"]), T.ldd[:, C:2 * C]).then_inc(S.ybs, 1)
+
+    g.sync.wait_ge(S.ybs, 8)
+    g.sync.dma_start(T.y[:], T.yb[:]).then_inc(S.st, 16)
+    g.sync.wait_ge(S.st, 16)

@@ -5,53 +5,38 @@ W = KT * C
 
 SCRATCH = {
     "xs": ("sbuf", [128, W], "bfloat16"),
-    "xp": ("sbuf", [128, W], "bfloat16"),
-    "xn0": ("sbuf", [128, W], "bfloat16"),
-    "xn1": ("sbuf", [128, W], "bfloat16"),
-    "sam": ("sbuf", [128, 2 * C], "bfloat16"),
-    "sd": ("sbuf", [128, 2 * C], "bfloat16"),
-    "lam": ("sbuf", [128, 2 * C], "bfloat16"),
-    "ldd": ("sbuf", [128, 2 * C], "bfloat16"),
+    "xm": ("sbuf", [128, W], "bfloat16"),
+    "xk": ("sbuf", [128, W], "bfloat16"),
+    "xrs": ("sbuf", [128, W], "bfloat16"),
+    "xro": ("sbuf", [128, W], "bfloat16"),
+    "sf": ("sbuf", [128, 3 * C], "bfloat16"),
     "yb": ("sbuf", [128, 8 * C], "bfloat16"),
-    "pam": ("psum", [128, 512], "float32"),
-    "pd0": ("psum", [128, 512], "float32"),
-    "pd1": ("psum", [128, 512], "float32"),
+    "pf0": ("psum", [128, 512], "float32"),
+    "pf1": ("psum", [128, 512], "float32"),
+    "pf2": ("psum", [128, 512], "float32"),
     "po0": ("psum", [128, 512], "float32"),
     "po1": ("psum", [128, 512], "float32"),
     "po2": ("psum", [128, 512], "float32"),
+    "po3": ("psum", [128, 512], "float32"),
 }
-SEMAPHORES = ["ld", "sb", "sa", "snt", "mam", "md0", "md1", "mo0", "mo1", "mo2", "cam", "cd", "sg1", "sg2", "ybs", "st"]
+SEMAPHORES = ["ld", "sk", "sm", "srs", "sro", "snt", "mf0", "mf1", "mf2", "mo0", "mo1", "mo2", "mo3",
+              "cf0", "cf12", "sg", "ybs", "st"]
 
 
 def _plan(core, cores, topo):
-    hosts = sorted({topo.host(c) for c in cores})
-    chips = sorted({topo.chip(c) for c in cores})
-    at = {(topo.host(c), topo.chip(c)): c for c in cores}
-
-    def linked(a, b):
-        return a != b and all(topo.may_write(at[(a, k)], at[(b, k)]) for k in chips)
-
-    ring = [hosts[0]]
-    ring.append([h for h in hosts if linked(ring[0], h) and topo.rack(h) == topo.rack(ring[0])][0])
-    while len(ring) < len(hosts):
-        ring.append([h for h in hosts if linked(ring[-1], h) and h not in ring][0])
-    i = ring.index(topo.host(core))
-    nxt, prv, far = ring[(i + 1) % len(ring)], ring[i - 1], ring[(i + 2) % len(ring)]
-    me_h, c = topo.host(core), topo.chip(core)
-    oc = [k for k in chips if k != c][0]
+    others = [s for s in cores if s != core]
+    rack = [s for s in others if topo.host(s) != topo.host(core) and topo.rack(topo.host(s)) == topo.rack(topo.host(core))]
+    cabled = [s for s in others if topo.rack(topo.host(s)) != topo.rack(topo.host(core)) and topo.may_write(core, s)]
     return {
-        "slot": chips.index(c),
-        "prev_same": at[(prv, c)], "prev_other": at[(prv, oc)],
-        "next_same": at[(nxt, c)], "next_other": at[(nxt, oc)],
-        "next_lo": at[(nxt, chips[0])], "next_hi": at[(nxt, chips[1])],
-        "far_lo": at[(far, chips[0])], "far_hi": at[(far, chips[1])],
-        "mate": at[(me_h, oc)],
+        "mate": [s for s in others if topo.mates(core, s)][0],
+        "rs": [s for s in rack if topo.same_plane(core, s)][0],
+        "ro": [s for s in rack if not topo.same_plane(core, s)][0],
+        "k": [s for s in cabled if topo.chip(s) == topo.chip(core)][0],
     }
 
 
 def rank_program(g, core, T, topo):
-    rank = T.rank_of(core)
-    if rank is None:
+    if T.rank_of(core) is None:
         return
     p = _plan(core, list(T.cores), topo)
     S = T.sem
@@ -68,69 +53,67 @@ def rank_program(g, core, T, topo):
             m = g.tensor.matmul(out, tile(a, t), tile(b, t), t == 0, t == KT - 1)
         m.then_inc(sem, 1)
 
-    def send(dst, out_ap, in_ap, sem):
-        rid, pid = topo.addr(dst, core)
-        g.remote_dma(out_ap, in_ap, sem, S.snt, pid, rid, topo.mask(core, dst))
-        return bin(topo.mask(core, dst)).count("1")
+    def dst(d):
+        rid, pid = topo.addr(d, core)
+        return DstId(rid=rid, pnc=pid)
+
+    common = topo.mask(core, p["mate"]) & topo.mask(core, p["rs"]) & topo.mask(core, p["ro"]) & topo.mask(core, p["k"])
+    eng = [b for b in range(16) if (common >> b) & 1]
+    NE = len(eng)
+
+    def group(i, n):
+        w = NE // n
+        return sum(1 << b for b in eng[i * w:(i + 1) * w])
 
     g.sync.dma_start(T.xs[:], T.x[:]).then_inc(S.ld, 16)
 
     g.wait_ge(S.ld, 16)
-    mine = T.xn0 if p["slot"] == 0 else T.xn1
-    back = [p["prev_same"], p["prev_other"]]
-    m_back = topo.mask(core, back[0]) & topo.mask(core, back[1])
-    ids = []
-    for d in back:
-        rid, pid = topo.addr(d, core)
-        ids.append(DstId(rid=rid, pnc=pid))
-    g.remote_dma_fused([RemoteDMATransfer(dst_ids=ids, dma_engine_mask=m_back, remote_sem=S.sb,
-                                          srcs=[T.xs[:]], dsts=[mine[:], mine[:]], alu_op=0)], local_sem=S.snt)
-    left = bin(m_back).count("1")
-    left += send(p["next_same"], T.xp[:], T.xs[:], S.sa)
-    g.wait_ge(S.cam, 1)
-    left += send(p["next_other"], T.lam[:], T.sam[:], S.sg1)
-    g.wait_ge(S.cd, 2)
-    left += send(p["prev_same"], T.ldd[:], T.sd[:], S.sg2)
-    g.wait_ge(S.snt, left)
+    ways = [(p["ro"], T.xro, S.sro), (p["rs"], T.xrs, S.srs), (p["k"], T.xk, S.sk), (p["mate"], T.xm, S.sm)]
+    g.remote_dma_fused([RemoteDMATransfer(dst_ids=[dst(d)], dma_engine_mask=group(i, 4), remote_sem=sem,
+                                          src=T.xs[:], dst=buf[:]) for i, (d, buf, sem) in enumerate(ways)],
+                       local_sem=S.snt)
+    there = yblk(p["k"])
+    g.wait_ge(S.cf0, 1)
+    g.remote_dma_fused([RemoteDMATransfer(dst_ids=[dst(p["mate"])], dma_engine_mask=group(0, 1), remote_sem=S.sg,
+                                          src=T.sf[:, 0:C], dst=there)], local_sem=S.snt)
+    g.wait_ge(S.cf12, 2)
+    g.remote_dma_fused([RemoteDMATransfer(dst_ids=[dst(d)], dma_engine_mask=group(i, 2), remote_sem=S.sg,
+                                          src=T.sf[:, C * (i + 1):C * (i + 2)], dst=there)
+                        for i, d in enumerate([p["rs"], p["ro"]])], local_sem=S.snt)
+    g.wait_ge(S.snt, 3 * NE)
 
-    def n_in(src):
-        return bin(topo.mask(src, core)).count("1")
-    in_b = 2 * bin(topo.mask(p["next_lo"], core) & topo.mask(p["next_hi"], core)).count("1")
-
-    x_no = T.xn0 if p["next_other"] == p["next_lo"] else T.xn1
-    x_ns = T.xn0 if p["next_same"] == p["next_lo"] else T.xn1
-    g.tensor.wait_ge(S.ld, 16)
-    g.tensor.wait_ge(S.sb, in_b)
-    gram(T.pam[:, 0:C], x_no, T.xs, S.mam)
-    gram(T.pam[:, C:2 * C], x_no, x_ns, S.mam)
-    g.tensor.wait_ge(S.sa, n_in(p["prev_same"]))
-    gram(T.pd0[:, 0:C], T.xp, T.xn0, S.md0)
-    gram(T.pd1[:, 0:C], T.xp, T.xn1, S.md1)
-    gram(T.po0[:, 0:C], T.xs, T.xn0, S.mo0)
-    gram(T.po1[:, 0:C], T.xs, T.xn1, S.mo1)
-    gram(T.po2[:, 0:C], T.xs, T.xp, S.mo2)
+    te = g.tensor
+    te.wait_ge(S.sk, NE // 4)
+    te.wait_ge(S.sm, NE // 4)
+    gram(T.pf0[:, 0:C], T.xm, T.xk, S.mf0)
+    te.wait_ge(S.srs, NE // 4)
+    gram(T.pf1[:, 0:C], T.xrs, T.xk, S.mf1)
+    te.wait_ge(S.sro, NE // 4)
+    gram(T.pf2[:, 0:C], T.xro, T.xk, S.mf2)
+    te.wait_ge(S.ld, 16)
+    gram(T.po0[:, 0:C], T.xs, T.xm, S.mo0)
+    gram(T.po1[:, 0:C], T.xs, T.xk, S.mo1)
+    gram(T.po2[:, 0:C], T.xs, T.xrs, S.mo2)
+    gram(T.po3[:, 0:C], T.xs, T.xro, S.mo3)
 
     v = g.vector
     v.memset(yblk(core), 0.0).then_inc(S.ybs, 1)
-    v.wait_ge(S.mam, 2)
-    v.tensor_copy(T.sam[:], T.pam[:, 0:2 * C]).then_inc(S.cam, 1)
-    v.wait_ge(S.md0, 1)
-    v.tensor_copy(T.sd[:, 0:C], T.pd0[:, 0:C]).then_inc(S.cd, 1)
-    v.wait_ge(S.md1, 1)
-    v.tensor_copy(T.sd[:, C:2 * C], T.pd1[:, 0:C]).then_inc(S.cd, 1)
+    v.wait_ge(S.mf0, 1)
+    v.tensor_copy(T.sf[:, 0:C], T.pf0[:, 0:C]).then_inc(S.cf0, 1)
+    v.wait_ge(S.mf1, 1)
+    v.tensor_copy(T.sf[:, C:2 * C], T.pf1[:, 0:C]).then_inc(S.cf12, 1)
+    v.wait_ge(S.mf2, 1)
+    v.tensor_copy(T.sf[:, 2 * C:3 * C], T.pf2[:, 0:C]).then_inc(S.cf12, 1)
     v.wait_ge(S.mo0, 1)
-    v.tensor_copy(yblk(p["next_lo"]), T.po0[:, 0:C]).then_inc(S.ybs, 1)
+    v.tensor_copy(yblk(p["mate"]), T.po0[:, 0:C]).then_inc(S.ybs, 1)
     v.wait_ge(S.mo1, 1)
-    v.tensor_copy(yblk(p["next_hi"]), T.po1[:, 0:C]).then_inc(S.ybs, 1)
+    v.tensor_copy(yblk(p["k"]), T.po1[:, 0:C]).then_inc(S.ybs, 1)
     v.wait_ge(S.mo2, 1)
-    v.tensor_copy(yblk(p["prev_same"]), T.po2[:, 0:C]).then_inc(S.ybs, 1)
-    v.wait_ge(S.sg1, n_in(p["prev_other"]))
-    v.tensor_copy(yblk(p["prev_other"]), T.lam[:, 0:C]).then_inc(S.ybs, 1)
-    v.tensor_copy(yblk(p["mate"]), T.lam[:, C:2 * C]).then_inc(S.ybs, 1)
-    v.wait_ge(S.sg2, n_in(p["next_same"]))
-    v.tensor_copy(yblk(p["far_lo"]), T.ldd[:, 0:C]).then_inc(S.ybs, 1)
-    v.tensor_copy(yblk(p["far_hi"]), T.ldd[:, C:2 * C]).then_inc(S.ybs, 1)
+    v.tensor_copy(yblk(p["rs"]), T.po2[:, 0:C]).then_inc(S.ybs, 1)
+    v.wait_ge(S.mo3, 1)
+    v.tensor_copy(yblk(p["ro"]), T.po3[:, 0:C]).then_inc(S.ybs, 1)
 
-    g.sync.wait_ge(S.ybs, 8)
+    g.sync.wait_ge(S.ybs, 5)
+    g.sync.wait_ge(S.sg, 2 * NE)
     g.sync.dma_start(T.y[:], T.yb[:]).then_inc(S.st, 16)
     g.sync.wait_ge(S.st, 16)

@@ -2,6 +2,8 @@ from concourse.bass import DstId, RemoteDMATransfer
 
 KT, C = 4, 128
 W = KT * C
+H = W // 2
+TH = KT // 2
 
 SCRATCH = {
     "xs": ("sbuf", [128, W], "bfloat16"),
@@ -19,8 +21,9 @@ SCRATCH = {
     "po2": ("psum", [128, 512], "float32"),
     "po3": ("psum", [128, 512], "float32"),
 }
-SEMAPHORES = ["ld", "sk", "sm", "srs", "sro", "snt", "mf0", "mf1", "mf2", "mo0", "mo1", "mo2", "mo3",
-              "cf0", "cf12", "sg", "ybs", "st"]
+SEMAPHORES = ["ld0", "ld1", "sk0", "sm0", "srs0", "sro0", "sk1", "sm1", "srs1", "sro1", "snt",
+              "mf0", "mf1", "mf2", "mo0", "mo1", "mo2", "mo3", "cf0", "cf12", "co0", "co1", "co2", "co3",
+              "sgm", "sgr", "st", "sto"]
 
 
 def _plan(core, cores, topo):
@@ -38,20 +41,19 @@ def _plan(core, cores, topo):
 def rank_program(g, core, T, topo):
     if T.rank_of(core) is None:
         return
-    p = _plan(core, list(T.cores), topo)
+    cores = list(T.cores)
+    p = _plan(core, cores, topo)
     S = T.sem
 
     def tile(buf, t):
         return buf[:, C * t:C * t + C]
 
-    def yblk(c):
-        r = T.rank_of(c)
-        return T.yb[:, C * r:C * r + C]
+    def half(buf, hf):
+        return buf[:, H * hf:H * hf + H]
 
-    def gram(out, a, b, sem):
-        for t in range(KT):
-            m = g.tensor.matmul(out, tile(a, t), tile(b, t), t == 0, t == KT - 1)
-        m.then_inc(sem, 1)
+    def blk(buf, c):
+        r = T.rank_of(c)
+        return buf[:, C * r:C * r + C]
 
     def dst(d):
         rid, pid = topo.addr(d, core)
@@ -65,55 +67,65 @@ def rank_program(g, core, T, topo):
         w = NE // n
         return sum(1 << b for b in eng[i * w:(i + 1) * w])
 
-    g.sync.dma_start(T.xs[:], T.x[:]).then_inc(S.ld, 16)
+    g.sync.dma_start(half(T.xs, 0), half(T.x, 0)).then_inc(S.ld0, 16)
+    g.scalar.dma_start(half(T.xs, 1), half(T.x, 1)).then_inc(S.ld1, 16)
 
-    g.wait_ge(S.ld, 16)
-    ways = [(p["ro"], T.xro, S.sro), (p["rs"], T.xrs, S.srs), (p["k"], T.xk, S.sk), (p["mate"], T.xm, S.sm)]
-    g.remote_dma_fused([RemoteDMATransfer(dst_ids=[dst(d)], dma_engine_mask=group(i, 4), remote_sem=sem,
-                                          src=T.xs[:], dst=buf[:]) for i, (d, buf, sem) in enumerate(ways)],
-                       local_sem=S.snt)
-    there = yblk(p["k"])
+    ways = [(p["ro"], T.xro, "sro"), (p["rs"], T.xrs, "srs"), (p["k"], T.xk, "sk"), (p["mate"], T.xm, "sm")]
+    for hf in range(2):
+        g.wait_ge(S["ld%d" % hf], 16)
+        g.remote_dma_fused([RemoteDMATransfer(dst_ids=[dst(d)], dma_engine_mask=group(i, 4), remote_sem=S["%s%d" % (nm, hf)],
+                                              src=half(T.xs, hf), dst=half(buf, hf)) for i, (d, buf, nm) in enumerate(ways)],
+                           local_sem=S.snt)
+    there = blk(T.yb, p["k"])
     g.wait_ge(S.cf0, 1)
-    g.remote_dma_fused([RemoteDMATransfer(dst_ids=[dst(p["mate"])], dma_engine_mask=group(0, 1), remote_sem=S.sg,
+    g.remote_dma_fused([RemoteDMATransfer(dst_ids=[dst(p["mate"])], dma_engine_mask=group(0, 1), remote_sem=S.sgm,
                                           src=T.sf[:, 0:C], dst=there)], local_sem=S.snt)
     g.wait_ge(S.cf12, 2)
-    g.remote_dma_fused([RemoteDMATransfer(dst_ids=[dst(d)], dma_engine_mask=group(i, 2), remote_sem=S.sg,
+    g.remote_dma_fused([RemoteDMATransfer(dst_ids=[dst(d)], dma_engine_mask=group(i, 2), remote_sem=S.sgr,
                                           src=T.sf[:, C * (i + 1):C * (i + 2)], dst=there)
                         for i, d in enumerate([p["rs"], p["ro"]])], local_sem=S.snt)
-    g.wait_ge(S.snt, 3 * NE)
+    g.wait_ge(S.snt, 4 * NE)
 
     te = g.tensor
-    te.wait_ge(S.sk, NE // 4)
-    te.wait_ge(S.sm, NE // 4)
-    gram(T.pf0[:, 0:C], T.xm, T.xk, S.mf0)
-    te.wait_ge(S.srs, NE // 4)
-    gram(T.pf1[:, 0:C], T.xrs, T.xk, S.mf1)
-    te.wait_ge(S.sro, NE // 4)
-    gram(T.pf2[:, 0:C], T.xro, T.xk, S.mf2)
-    te.wait_ge(S.ld, 16)
-    gram(T.po0[:, 0:C], T.xs, T.xm, S.mo0)
-    gram(T.po1[:, 0:C], T.xs, T.xk, S.mo1)
-    gram(T.po2[:, 0:C], T.xs, T.xrs, S.mo2)
-    gram(T.po3[:, 0:C], T.xs, T.xro, S.mo3)
+    Q = NE // 4
+    jobs = [(T.pf0, T.xm, T.xk, S.mf0, ["sk", "sm"]),
+            (T.pf1, T.xrs, T.xk, S.mf1, ["srs"]),
+            (T.pf2, T.xro, T.xk, S.mf2, ["sro"]),
+            (T.po0, T.xs, T.xm, S.mo0, ["ld"]),
+            (T.po1, T.xs, T.xk, S.mo1, []),
+            (T.po2, T.xs, T.xrs, S.mo2, []),
+            (T.po3, T.xs, T.xro, S.mo3, [])]
+    for hf in range(2):
+        for out, a, b, done, needs in jobs:
+            for nm in needs:
+                te.wait_ge(S["%s%d" % (nm, hf)], 16 if nm == "ld" else Q)
+            for t in range(TH * hf, TH * hf + TH):
+                m = te.matmul(out[:, 0:C], tile(a, t), tile(b, t), t == 0, t == KT - 1)
+            if hf == 1:
+                m.then_inc(done, 1)
 
     v = g.vector
-    v.memset(yblk(core), 0.0).then_inc(S.ybs, 1)
     v.wait_ge(S.mf0, 1)
     v.tensor_copy(T.sf[:, 0:C], T.pf0[:, 0:C]).then_inc(S.cf0, 1)
     v.wait_ge(S.mf1, 1)
     v.tensor_copy(T.sf[:, C:2 * C], T.pf1[:, 0:C]).then_inc(S.cf12, 1)
     v.wait_ge(S.mf2, 1)
     v.tensor_copy(T.sf[:, 2 * C:3 * C], T.pf2[:, 0:C]).then_inc(S.cf12, 1)
-    v.wait_ge(S.mo0, 1)
-    v.tensor_copy(yblk(p["mate"]), T.po0[:, 0:C]).then_inc(S.ybs, 1)
-    v.wait_ge(S.mo1, 1)
-    v.tensor_copy(yblk(p["k"]), T.po1[:, 0:C]).then_inc(S.ybs, 1)
-    v.wait_ge(S.mo2, 1)
-    v.tensor_copy(yblk(p["rs"]), T.po2[:, 0:C]).then_inc(S.ybs, 1)
-    v.wait_ge(S.mo3, 1)
-    v.tensor_copy(yblk(p["ro"]), T.po3[:, 0:C]).then_inc(S.ybs, 1)
+    own = [p["mate"], p["k"], p["rs"], p["ro"]]
+    for i, s in enumerate(own):
+        v.wait_ge(S["mo%d" % i], 1)
+        v.tensor_copy(blk(T.yb, s), T["po%d" % i][:, 0:C]).then_inc(S["co%d" % i], 1)
 
-    g.sync.wait_ge(S.ybs, 5)
-    g.sync.wait_ge(S.sg, 2 * NE)
-    g.sync.dma_start(T.y[:], T.yb[:]).then_inc(S.st, 16)
-    g.sync.wait_ge(S.st, 16)
+    for i, s in enumerate(own):
+        g.scalar.wait_ge(S["co%d" % i], 1)
+        g.scalar.dma_start(blk(T.y, s), blk(T.yb, s)).then_inc(S.sto, 16)
+    g.scalar.wait_ge(S.sto, 16 * len(own))
+
+    g.sync.wait_ge(S.sgm, NE)
+    late = _plan(p["mate"], cores, topo)["k"]
+    g.sync.dma_start(blk(T.y, late), blk(T.yb, late)).then_inc(S.st, 16)
+    g.sync.wait_ge(S.sgr, NE)
+    for s in (p["rs"], p["ro"]):
+        late = _plan(s, cores, topo)["k"]
+        g.sync.dma_start(blk(T.y, late), blk(T.yb, late)).then_inc(S.st, 16)
+    g.sync.wait_ge(S.st, 48)

@@ -3,7 +3,7 @@ from concourse.bass import DstId, RemoteDMATransfer
 KT, C = 4, 128
 W = KT * C
 H = W // 2
-TH = KT // 2
+WORLD = 512
 
 SCRATCH = {
     "xs": ("sbuf", [128, W], "bfloat16"),
@@ -21,7 +21,8 @@ SCRATCH = {
     "po2": ("psum", [128, 512], "float32"),
     "po3": ("psum", [128, 512], "float32"),
 }
-SEMAPHORES = ["ld0", "ld1", "sk0", "sm0", "srs0", "sro0", "sk1", "sm1", "srs1", "sro1", "snt",
+SEMAPHORES = ["ld0", "ld1", "hin", "snt",
+              "sk0", "sm0", "srs0", "sro0", "sk2", "sm2", "srs2", "sro2", "sk3", "sm3", "srs3", "sro3",
               "mf0", "mf1", "mf2", "mo0", "mo1", "mo2", "mo3", "cf0", "cf12", "co0", "co1", "co2", "co3",
               "sgm", "sgr", "st", "sto"]
 
@@ -30,26 +31,72 @@ def _plan(core, cores, topo):
     others = [s for s in cores if s != core]
     rack = [s for s in others if topo.host(s) != topo.host(core) and topo.rack(topo.host(s)) == topo.rack(topo.host(core))]
     cabled = [s for s in others if topo.rack(topo.host(s)) != topo.rack(topo.host(core)) and topo.may_write(core, s)]
+    mate = [s for s in others if topo.mates(core, s)][0]
+    chipmates = [c for c in range(WORLD) if c != core and topo.host(c) == topo.host(core) and topo.chip(c) == topo.chip(core)]
+    far = [c for c in chipmates if topo.die(c) != topo.die(core)]
+    near = [c for c in chipmates if topo.die(c) == topo.die(core)]
     return {
-        "mate": [s for s in others if topo.mates(core, s)][0],
+        "mate": mate,
         "rs": [s for s in rack if topo.same_plane(core, s)][0],
         "ro": [s for s in rack if not topo.same_plane(core, s)][0],
         "k": [s for s in cabled if topo.chip(s) == topo.chip(core)][0],
+        "ha": [c for c in far if topo.may_write(c, mate)][0],
+        "hc": [c for c in far if not topo.may_write(c, mate)][0],
+        "hb": [c for c in near if not topo.may_write(c, mate)][0],
     }
 
 
-def rank_program(g, core, T, topo):
-    if T.rank_of(core) is None:
-        return
-    cores = list(T.cores)
-    p = _plan(core, cores, topo)
+def _engines(m):
+    return [b for b in range(16) if (m >> b) & 1]
+
+
+def _mask(engs):
+    return sum(1 << b for b in engs)
+
+
+def tile(buf, t):
+    return buf[:, C * t:C * t + C]
+
+
+def _helper_program(g, core, T, topo, p, role):
     S = T.sem
 
-    def tile(buf, t):
-        return buf[:, C * t:C * t + C]
+    def dst(d):
+        rid, pid = topo.addr(d, core)
+        return DstId(rid=rid, pnc=pid)
 
-    def half(buf, hf):
-        return buf[:, H * hf:H * hf + H]
+    todo = {"ha": (3, [(p["mate"], T.xm, S.sm3), (p["ro"], T.xro, S.sro3)]),
+            "hc": (3, [(p["k"], T.xk, S.sk3), (p["rs"], T.xrs, S.srs3)]),
+            "hb": (2, [(p["k"], T.xk, S.sk2)])}
+    t, ways = todo[role]
+    m = topo.mask(core, ways[0][0])
+    for d, _, _ in ways:
+        m &= topo.mask(core, d)
+    eng = _engines(m)
+    w = len(eng) // 2
+    g.wait_ge(S.hin, HAND[role])
+    g.remote_dma_fused([RemoteDMATransfer(dst_ids=[dst(d)], dma_engine_mask=_mask(eng[i * w:(i + 1) * w]), remote_sem=sem,
+                                          src=tile(T.xs, t), dst=tile(buf, t)) for i, (d, buf, sem) in enumerate(ways)],
+                       local_sem=S.snt)
+    g.wait_ge(S.snt, w * len(ways))
+
+
+HAND = {"hc": 4, "ha": 2, "hb": 2}
+HTILE = {"hc": 3, "ha": 3, "hb": 2}
+
+
+def rank_program(g, core, T, topo):
+    cores = list(T.cores)
+    if T.rank_of(core) is None:
+        for r in cores:
+            if topo.host(r) == topo.host(core) and topo.chip(r) == topo.chip(core):
+                pr = _plan(r, cores, topo)
+                for role in ("ha", "hb", "hc"):
+                    if pr[role] == core:
+                        _helper_program(g, core, T, topo, pr, role)
+        return
+    p = _plan(core, cores, topo)
+    S = T.sem
 
     def blk(buf, c):
         r = T.rank_of(c)
@@ -60,22 +107,38 @@ def rank_program(g, core, T, topo):
         return DstId(rid=rid, pnc=pid)
 
     common = topo.mask(core, p["mate"]) & topo.mask(core, p["rs"]) & topo.mask(core, p["ro"]) & topo.mask(core, p["k"])
-    eng = [b for b in range(16) if (common >> b) & 1]
+    eng = _engines(common)
     NE = len(eng)
+    home = _engines(topo.mask(core, p["ha"]) & topo.mask(core, p["hb"]) & topo.mask(core, p["hc"]) & ~common)
 
     def group(i, n):
         w = NE // n
-        return sum(1 << b for b in eng[i * w:(i + 1) * w])
+        return _mask(eng[i * w:(i + 1) * w])
 
-    g.sync.dma_start(half(T.xs, 0), half(T.x, 0)).then_inc(S.ld0, 16)
-    g.scalar.dma_start(half(T.xs, 1), half(T.x, 1)).then_inc(S.ld1, 16)
+    g.sync.dma_start(T.xs[:, H:W], T.x[:, H:W]).then_inc(S.ld1, 16)
+    g.scalar.dma_start(T.xs[:, 0:H], T.x[:, 0:H]).then_inc(S.ld0, 16)
 
+    sent = 0
+    g.wait_ge(S.ld1, 16)
+    hand, at = [], 0
+    for role in ("hc", "ha", "hb"):
+        n = HAND[role]
+        hand.append(RemoteDMATransfer(dst_ids=[dst(p[role])], dma_engine_mask=_mask(home[at:at + n]), remote_sem=S.hin,
+                                      src=tile(T.xs, HTILE[role]), dst=tile(T.xs, HTILE[role])))
+        at += n
+        sent += n
+    g.remote_dma_fused(hand, local_sem=S.snt)
     ways = [(p["ro"], T.xro, "sro"), (p["rs"], T.xrs, "srs"), (p["k"], T.xk, "sk"), (p["mate"], T.xm, "sm")]
-    for hf in range(2):
-        g.wait_ge(S["ld%d" % hf], 16)
-        g.remote_dma_fused([RemoteDMATransfer(dst_ids=[dst(d)], dma_engine_mask=group(i, 4), remote_sem=S["%s%d" % (nm, hf)],
-                                              src=half(T.xs, hf), dst=half(buf, hf)) for i, (d, buf, nm) in enumerate(ways)],
-                           local_sem=S.snt)
+    Q = NE // 4
+    g.wait_ge(S.ld0, 16)
+    g.remote_dma_fused([RemoteDMATransfer(dst_ids=[dst(d)], dma_engine_mask=group(i, 4), remote_sem=S[nm + "0"],
+                                          src=T.xs[:, 0:H], dst=buf[:, 0:H]) for i, (d, buf, nm) in enumerate(ways)],
+                       local_sem=S.snt)
+    sent += NE
+    g.remote_dma_fused([RemoteDMATransfer(dst_ids=[dst(d)], dma_engine_mask=group(i, 4), remote_sem=S[nm + "2"],
+                                          src=tile(T.xs, 2), dst=tile(buf, 2)) for i, (d, buf, nm) in enumerate(ways)
+                        if nm != "sk"], local_sem=S.snt)
+    sent += 3 * Q
     there = blk(T.yb, p["k"])
     g.wait_ge(S.cf0, 1)
     g.remote_dma_fused([RemoteDMATransfer(dst_ids=[dst(p["mate"])], dma_engine_mask=group(0, 1), remote_sem=S.sgm,
@@ -84,25 +147,36 @@ def rank_program(g, core, T, topo):
     g.remote_dma_fused([RemoteDMATransfer(dst_ids=[dst(d)], dma_engine_mask=group(i, 2), remote_sem=S.sgr,
                                           src=T.sf[:, C * (i + 1):C * (i + 2)], dst=there)
                         for i, d in enumerate([p["rs"], p["ro"]])], local_sem=S.snt)
-    g.wait_ge(S.snt, 4 * NE)
+    sent += 2 * NE
+    g.wait_ge(S.snt, sent)
 
     te = g.tensor
-    Q = NE // 4
-    jobs = [(T.pf0, T.xm, T.xk, S.mf0, ["sk", "sm"]),
-            (T.pf1, T.xrs, T.xk, S.mf1, ["srs"]),
-            (T.pf2, T.xro, T.xk, S.mf2, ["sro"]),
-            (T.po0, T.xs, T.xm, S.mo0, ["ld"]),
-            (T.po1, T.xs, T.xk, S.mo1, []),
-            (T.po2, T.xs, T.xrs, S.mo2, []),
-            (T.po3, T.xs, T.xro, S.mo3, [])]
-    for hf in range(2):
-        for out, a, b, done, needs in jobs:
+    HW_ = NE // 2
+    foreign = [(T.pf0, T.xm, T.xk, S.mf0, ["sk", "sm"]),
+               (T.pf1, T.xrs, T.xk, S.mf1, ["srs"]),
+               (T.pf2, T.xro, T.xk, S.mf2, ["sro"])]
+    mine = [(T.po0, T.xs, T.xm, S.mo0), (T.po1, T.xs, T.xk, S.mo1), (T.po2, T.xs, T.xrs, S.mo2), (T.po3, T.xs, T.xro, S.mo3)]
+    for out, a, b, done, needs in foreign:
+        for nm in needs:
+            te.wait_ge(S[nm + "0"], Q)
+        for t in (0, 1):
+            te.matmul(out[:, 0:C], tile(a, t), tile(b, t), t == 0, False)
+    te.wait_ge(S.ld0, 16)
+    for out, a, b, done in mine:
+        for t in (0, 1):
+            te.matmul(out[:, 0:C], tile(a, t), tile(b, t), t == 0, False)
+    for t in (2, 3):
+        for out, a, b, done, needs in foreign:
             for nm in needs:
-                te.wait_ge(S["%s%d" % (nm, hf)], 16 if nm == "ld" else Q)
-            for t in range(TH * hf, TH * hf + TH):
-                m = te.matmul(out[:, 0:C], tile(a, t), tile(b, t), t == 0, t == KT - 1)
-            if hf == 1:
+                te.wait_ge(S["%s%d" % (nm, t)], HW_ if (t == 3 or nm == "sk") else Q)
+            m = te.matmul(out[:, 0:C], tile(a, t), tile(b, t), False, t == KT - 1)
+            if t == KT - 1:
                 m.then_inc(done, 1)
+    te.wait_ge(S.ld1, 16)
+    for out, a, b, done in mine:
+        for t in (2, 3):
+            m = te.matmul(out[:, 0:C], tile(a, t), tile(b, t), False, t == KT - 1)
+        m.then_inc(done, 1)
 
     v = g.vector
     v.wait_ge(S.mf0, 1)

from concourse.bass import DstId, RemoteDMATransfer

KT, C = 4, 128
W = KT * C
H = W // 2
WORLD = 512

SCRATCH = {
    "xs": ("sbuf", [128, W], "bfloat16"),
    "xm": ("sbuf", [128, W], "bfloat16"),
    "xk": ("sbuf", [128, W], "bfloat16"),
    "xrs": ("sbuf", [128, W], "bfloat16"),
    "xro": ("sbuf", [128, W], "bfloat16"),
    "sf": ("sbuf", [128, 3 * C], "bfloat16"),
    "yb": ("sbuf", [128, 8 * C], "bfloat16"),
    "pf0": ("psum", [128, 512], "float32"),
    "pf1": ("psum", [128, 512], "float32"),
    "pf2": ("psum", [128, 512], "float32"),
    "po0": ("psum", [128, 512], "float32"),
    "po1": ("psum", [128, 512], "float32"),
    "po2": ("psum", [128, 512], "float32"),
    "po3": ("psum", [128, 512], "float32"),
}
SEMAPHORES = ["ld0", "ld1", "hin", "snt",
              "sk0", "sm0", "srs0", "sro0", "sk2", "sm2", "srs2", "sro2", "sk3", "sm3", "srs3", "sro3",
              "mf0", "mf1", "mf2", "mo0", "mo1", "mo2", "mo3", "cf0", "cf12", "co0", "co1", "co2", "co3",
              "sgm", "sgr", "st", "sto"]


def _plan(core, cores, topo):
    others = [s for s in cores if s != core]
    rack = [s for s in others if topo.host(s) != topo.host(core) and topo.rack(topo.host(s)) == topo.rack(topo.host(core))]
    cabled = [s for s in others if topo.rack(topo.host(s)) != topo.rack(topo.host(core)) and topo.may_write(core, s)]
    mate = [s for s in others if topo.mates(core, s)][0]
    chipmates = [c for c in range(WORLD) if c != core and topo.host(c) == topo.host(core) and topo.chip(c) == topo.chip(core)]
    far = [c for c in chipmates if topo.die(c) != topo.die(core)]
    near = [c for c in chipmates if topo.die(c) == topo.die(core)]
    return {
        "mate": mate,
        "rs": [s for s in rack if topo.same_plane(core, s)][0],
        "ro": [s for s in rack if not topo.same_plane(core, s)][0],
        "k": [s for s in cabled if topo.chip(s) == topo.chip(core)][0],
        "ha": [c for c in far if topo.may_write(c, mate)][0],
        "hc": [c for c in far if not topo.may_write(c, mate)][0],
        "hb": [c for c in near if not topo.may_write(c, mate)][0],
    }


def _engines(m):
    return [b for b in range(16) if (m >> b) & 1]


def _mask(engs):
    return sum(1 << b for b in engs)


def tile(buf, t):
    return buf[:, C * t:C * t + C]


def _helper_program(g, core, T, topo, p, role):
    S = T.sem

    def dst(d):
        rid, pid = topo.addr(d, core)
        return DstId(rid=rid, pnc=pid)

    todo = {"ha": (3, [(p["mate"], T.xm, S.sm3), (p["ro"], T.xro, S.sro3)]),
            "hc": (3, [(p["k"], T.xk, S.sk3), (p["rs"], T.xrs, S.srs3)]),
            "hb": (2, [(p["k"], T.xk, S.sk2)])}
    t, ways = todo[role]
    m = topo.mask(core, ways[0][0])
    for d, _, _ in ways:
        m &= topo.mask(core, d)
    eng = _engines(m)
    w = len(eng) // 2
    g.wait_ge(S.hin, HAND[role])
    g.remote_dma_fused([RemoteDMATransfer(dst_ids=[dst(d)], dma_engine_mask=_mask(eng[i * w:(i + 1) * w]), remote_sem=sem,
                                          src=tile(T.xs, t), dst=tile(buf, t)) for i, (d, buf, sem) in enumerate(ways)],
                       local_sem=S.snt)
    g.wait_ge(S.snt, w * len(ways))


HAND = {"hc": 4, "ha": 2, "hb": 2}
HTILE = {"hc": 3, "ha": 3, "hb": 2}


def rank_program(g, core, T, topo):
    cores = list(T.cores)
    if T.rank_of(core) is None:
        for r in cores:
            if topo.host(r) == topo.host(core) and topo.chip(r) == topo.chip(core):
                pr = _plan(r, cores, topo)
                for role in ("ha", "hb", "hc"):
                    if pr[role] == core:
                        _helper_program(g, core, T, topo, pr, role)
        return
    p = _plan(core, cores, topo)
    S = T.sem

    def blk(buf, c):
        r = T.rank_of(c)
        return buf[:, C * r:C * r + C]

    def dst(d):
        rid, pid = topo.addr(d, core)
        return DstId(rid=rid, pnc=pid)

    common = topo.mask(core, p["mate"]) & topo.mask(core, p["rs"]) & topo.mask(core, p["ro"]) & topo.mask(core, p["k"])
    eng = _engines(common)
    NE = len(eng)
    home = _engines(topo.mask(core, p["ha"]) & topo.mask(core, p["hb"]) & topo.mask(core, p["hc"]) & ~common)

    def group(i, n):
        w = NE // n
        return _mask(eng[i * w:(i + 1) * w])

    g.sync.dma_start(T.xs[:, H:W], T.x[:, H:W]).then_inc(S.ld1, 16)
    g.scalar.dma_start(T.xs[:, 0:H], T.x[:, 0:H]).then_inc(S.ld0, 16)

    sent = 0
    g.wait_ge(S.ld1, 16)
    hand, at = [], 0
    for role in ("hc", "ha", "hb"):
        n = HAND[role]
        hand.append(RemoteDMATransfer(dst_ids=[dst(p[role])], dma_engine_mask=_mask(home[at:at + n]), remote_sem=S.hin,
                                      src=tile(T.xs, HTILE[role]), dst=tile(T.xs, HTILE[role])))
        at += n
        sent += n
    g.remote_dma_fused(hand, local_sem=S.snt)
    ways = [(p["ro"], T.xro, "sro"), (p["rs"], T.xrs, "srs"), (p["k"], T.xk, "sk"), (p["mate"], T.xm, "sm")]
    Q = NE // 4
    g.wait_ge(S.ld0, 16)
    g.remote_dma_fused([RemoteDMATransfer(dst_ids=[dst(d)], dma_engine_mask=group(i, 4), remote_sem=S[nm + "0"],
                                          src=T.xs[:, 0:H], dst=buf[:, 0:H]) for i, (d, buf, nm) in enumerate(ways)],
                       local_sem=S.snt)
    sent += NE
    g.remote_dma_fused([RemoteDMATransfer(dst_ids=[dst(d)], dma_engine_mask=group(i, 4), remote_sem=S[nm + "2"],
                                          src=tile(T.xs, 2), dst=tile(buf, 2)) for i, (d, buf, nm) in enumerate(ways)
                        if nm != "sk"], local_sem=S.snt)
    sent += 3 * Q
    there = blk(T.yb, p["k"])
    g.wait_ge(S.cf0, 1)
    g.remote_dma_fused([RemoteDMATransfer(dst_ids=[dst(p["mate"])], dma_engine_mask=group(0, 1), remote_sem=S.sgm,
                                          src=T.sf[:, 0:C], dst=there)], local_sem=S.snt)
    g.wait_ge(S.cf12, 2)
    g.remote_dma_fused([RemoteDMATransfer(dst_ids=[dst(d)], dma_engine_mask=group(i, 2), remote_sem=S.sgr,
                                          src=T.sf[:, C * (i + 1):C * (i + 2)], dst=there)
                        for i, d in enumerate([p["rs"], p["ro"]])], local_sem=S.snt)
    sent += 2 * NE
    g.wait_ge(S.snt, sent)

    te = g.tensor
    HW_ = NE // 2
    foreign = [(T.pf0, T.xm, T.xk, S.mf0, ["sk", "sm"]),
               (T.pf1, T.xrs, T.xk, S.mf1, ["srs"]),
               (T.pf2, T.xro, T.xk, S.mf2, ["sro"])]
    mine = [(T.po0, T.xs, T.xm, S.mo0), (T.po1, T.xs, T.xk, S.mo1), (T.po2, T.xs, T.xrs, S.mo2), (T.po3, T.xs, T.xro, S.mo3)]
    for out, a, b, done, needs in foreign:
        for nm in needs:
            te.wait_ge(S[nm + "0"], Q)
        for t in (0, 1):
            te.matmul(out[:, 0:C], tile(a, t), tile(b, t), t == 0, False)
    te.wait_ge(S.ld0, 16)
    for out, a, b, done in mine:
        for t in (0, 1):
            te.matmul(out[:, 0:C], tile(a, t), tile(b, t), t == 0, False)
    for t in (2, 3):
        for out, a, b, done, needs in foreign:
            for nm in needs:
                te.wait_ge(S["%s%d" % (nm, t)], HW_ if (t == 3 or nm == "sk") else Q)
            m = te.matmul(out[:, 0:C], tile(a, t), tile(b, t), False, t == KT - 1)
            if t == KT - 1:
                m.then_inc(done, 1)
    te.wait_ge(S.ld1, 16)
    for out, a, b, done in mine:
        for t in (2, 3):
            m = te.matmul(out[:, 0:C], tile(a, t), tile(b, t), False, t == KT - 1)
        m.then_inc(done, 1)

    v = g.vector
    v.wait_ge(S.mf0, 1)
    v.tensor_copy(T.sf[:, 0:C], T.pf0[:, 0:C]).then_inc(S.cf0, 1)
    v.wait_ge(S.mf1, 1)
    v.tensor_copy(T.sf[:, C:2 * C], T.pf1[:, 0:C]).then_inc(S.cf12, 1)
    v.wait_ge(S.mf2, 1)
    v.tensor_copy(T.sf[:, 2 * C:3 * C], T.pf2[:, 0:C]).then_inc(S.cf12, 1)
    own = [p["mate"], p["k"], p["rs"], p["ro"]]
    for i, s in enumerate(own):
        v.wait_ge(S["mo%d" % i], 1)
        v.tensor_copy(blk(T.yb, s), T["po%d" % i][:, 0:C]).then_inc(S["co%d" % i], 1)

    for i, s in enumerate(own):
        g.scalar.wait_ge(S["co%d" % i], 1)
        g.scalar.dma_start(blk(T.y, s), blk(T.yb, s)).then_inc(S.sto, 16)
    g.scalar.wait_ge(S.sto, 16 * len(own))

    g.sync.wait_ge(S.sgm, NE)
    late = _plan(p["mate"], cores, topo)["k"]
    g.sync.dma_start(blk(T.y, late), blk(T.yb, late)).then_inc(S.st, 16)
    g.sync.wait_ge(S.sgr, NE)
    for s in (p["rs"], p["ro"]):
        late = _plan(s, cores, topo)["k"]
        g.sync.dma_start(blk(T.y, late), blk(T.yb, late)).then_inc(S.st, 16)
    g.sync.wait_ge(S.st, 48)
